import numpy as np
import ml_dtypes


def mxq(x, axis, fmt="e4m3"):
    dtype, down = {"e4m3": (ml_dtypes.float8_e4m3fn, 7), "e5m2": (ml_dtypes.float8_e5m2, 14)}[fmt]
    v = np.moveaxis(np.asarray(x, np.float32).astype(ml_dtypes.bfloat16).astype(np.float64), axis, -1)
    blocks = v.reshape(v.shape[:-1] + (-1, 32))
    amax = np.abs(blocks).max(-1, keepdims=True)
    byte = np.maximum(np.where(amax > 0, np.frexp(amax)[1] - 1 + 127, 0) - down, 1)
    scale = np.exp2(byte - 127.0)
    codes = (blocks / scale).astype(np.float32).astype(dtype).astype(np.float64)
    return np.moveaxis((codes * scale).reshape(v.shape), -1, axis)


WIDE = False


def mx_kscale(k):
    if not WIDE:
        return np.ones(k)
    levels = np.array([10, -10, 5, -5, 0])
    if k % 512:
        return np.exp2(np.random.permutation(np.resize(levels, k // 32))).repeat(32)
    a = np.empty((k // 512, 16))
    for p in range(k // 512):
        a[p, :8] = np.random.permutation(np.resize(levels, 8))
        for g in range(8):
            far = levels[np.abs(levels - a[p, g]) >= 10]
            a[p, g + 8] = far[np.random.randint(len(far))]
    return np.exp2(a.ravel()).repeat(32)


def f64(x):
    return np.asarray(x).astype(np.float64)


def striped(idx):
    return np.tile(np.asarray(idx).reshape(-1, 16).T, (8, 1)).astype(np.uint16)


def unstriped(offs):
    return offs[:16].T.reshape(-1).astype(np.int64)


E2M1 = np.array([0.0, 0.5, 1.0, 1.5, 2.0, 3.0, 4.0, 6.0, -0.0, -0.5, -1.0, -1.5, -2.0, -3.0, -4.0, -6.0])


def pack_weight(w, fmt):
    k, n = w.shape
    w = f64(np.asarray(w, np.float32).astype(ml_dtypes.bfloat16)).reshape(k // 32, 32, n)
    amax = np.abs(w).max(1)
    if fmt == "e4m3":
        byte = np.frexp(amax)[1] - 1 + 127 - 7
    else:
        mant, ex = np.frexp(amax / 6.0)
        byte = np.where(mant > 0.5, ex, ex - 1) + 127
    byte = np.clip(np.where(amax > 0, byte, 1), 1, 254)
    scaled = (w * np.exp2(127.0 - byte)[:, None, :]).reshape(k, n).astype(np.float32)
    by_word = np.ascontiguousarray(scaled.reshape(k // 512, 128, 4, n).transpose(0, 1, 3, 2))
    if fmt == "e4m3":
        words = by_word.astype(ml_dtypes.float8_e4m3fn).view(np.uint8)
    else:
        c = by_word.astype(ml_dtypes.float4_e2m1fn).view(np.uint8) & 0xF
        words = (c[..., 0::2] | (c[..., 1::2] << 4)).reshape(k // 512, 128, 2 * n)
    return np.ascontiguousarray(words), np.ascontiguousarray(byte.astype(np.uint8).reshape(k // 512, 16, n))


def unpack_weight(words, scales, fmt):
    g, _, n = scales.shape
    words = np.ascontiguousarray(words).reshape(g, 128, n, -1)
    if fmt == "e4m3":
        vals = words.view(ml_dtypes.float8_e4m3fn).astype(np.float64)
    else:
        nib = np.empty((g, 128, n, 4), np.uint8)
        nib[..., 0::2] = words & 0xF
        nib[..., 1::2] = words >> 4
        vals = E2M1[nib]
    vals = vals * np.repeat(np.exp2(scales.astype(np.float64) - 127.0), 8, axis=1)[..., None]
    return vals.transpose(0, 1, 3, 2).reshape(g * 512, n)


def sigmoid(v):
    return 1.0 / (1.0 + np.exp(-v))


def bf(x):
    return np.asarray(x, np.float32).astype(ml_dtypes.bfloat16)


def planes(Y):
    r, m = Y.shape
    b = f64(bf(Y)).reshape(r // 32, 32, m)
    amax = np.abs(b).max(1)
    byte = np.clip(np.where(amax > 0, np.frexp(amax)[1] - 1 + 127 - 7, 1), 1, 254)
    codes = (b * np.exp2(127.0 - byte)[:, None, :]).reshape(r, m).astype(np.float32).astype(ml_dtypes.float8_e4m3fn).view(np.uint8)
    words = codes.reshape(r // 512, 128, 4, m).transpose(0, 1, 3, 2)
    return np.ascontiguousarray(words), np.ascontiguousarray(byte.astype(np.uint8).reshape(r // 512, 16, m))


K, R, F, T, J, G = 512, 512, 512, 2048, 512, 128


def setup_inputs():
    n = np.random.standard_normal
    idx = np.random.permutation(T)[:J]
    fk = mx_kscale(K)
    ff = mx_kscale(F)
    tabp = pack_weight(n((K, T)) / fk[:, None], "e4m3")
    return {
        "tab_words": tabp[0],
        "tab_scales": tabp[1],
        "w1": (n((K, R)) * 1 / np.sqrt(K) * fk[:, None]).astype(np.float32),
        "temper": (np.random.uniform(0.5, 2.0, (R, 1))).astype(np.float32),
        "wo": (n((F, R)) * 1 / np.sqrt(F) * ff[:, None]).astype(np.float32),
        "dy": (n((F, G)) / ff[:, None]).astype(np.float32),
        "old": (0.5 * n((R, J))).astype(np.float32),
        "offs": striped(idx),
    }


def reference(tab_words, tab_scales, w1, temper, wo, dy, old, offs):
    idx = unstriped(offs)
    tabu = unpack_weight(tab_words, tab_scales, "e4m3")
    w1q = mxq(f64(w1), 0, "e4m3")
    tabidxg = tabu[:, idx]
    a = w1q.T @ tabidxg
    p = np.exp(a * f64(temper))
    z = p.reshape(R, G, J // G).sum(axis=2)
    s = np.log(z) / f64(temper)
    woq = mxq(f64(wo), 0, "e4m3")
    dyq = mxq(f64(dy), 0, "e4m3")
    c0 = woq.T @ dyq
    ds = c0 * sigmoid(s) * (1.0 + s * (1.0 - sigmoid(s)))
    dz = ds / f64(temper) / z
    r1 = np.repeat(dz, J // G, axis=1)
    da = r1 * p * f64(temper)
    y = da + f64(old)
    words, scales = planes(y)
    return y, words, scales

@@ -1,0 +1,202 @@
+from contextlib import ExitStack
+
+import concourse.mybir as mybir
+
+K, R, F, T, J, G = 512, 512, 512, 2048, 512, 128
+FLOPS = 2 * K * R * J + 2 * F * R * G
+
+F32 = mybir.dt.float32
+BF16 = mybir.dt.bfloat16
+I32 = mybir.dt.int32
+U32 = mybir.dt.uint32
+U16 = mybir.dt.uint16
+U8 = mybir.dt.uint8
+FP8X4 = mybir.dt.float8_e4m3fn_x4
+ALU = mybir.AluOpType
+ACT = mybir.ActivationFunctionType
+AX = mybir.AxisListType
+
+P = 128
+PACK = 4
+POOL = J // G
+HALF = J // 2
+GH = G // 2
+QUART = J // 4
+GQ = G // 4
+
+
+def tile_attend_csoftmaxpool_pl_kernel(tc, tab_words, tab_scales, w1, temper, wo, dy, old, offs, out_0, out_1, out_2):
+    nc = tc.nc
+    with ExitStack() as ctx:
+        sb = ctx.enter_context(tc.tile_pool(name="sb", bufs=1))
+        ps = ctx.enter_context(tc.psum_pool(name="ps", bufs=1))
+
+        offsets = sb.tile([P, J // 16], U16, name="offsets")
+        tabw = sb.tile([P, T], I32, name="tabw", align_bytes=64)
+        tabs = sb.tile([P, T], U8, name="tabs", align_bytes=64)
+        w1_raw = sb.tile([P, PACK, R], F32, name="w1_raw")
+        wo_raw = sb.tile([P, PACK, R], F32, name="wo_raw")
+        dy_raw = sb.tile([P, PACK, G], F32, name="dy_raw")
+        old_sb = sb.tile([P, PACK, J], F32, name="old_sb")
+        temp = sb.tile([P, PACK], F32, name="temp")
+
+        nc.vector.memset(tabs[:].bitcast(I32), 0)
+        nc.sync.dma_start(w1_raw[:], w1.rearrange("(p j) c -> p j c", j=PACK))
+        nc.sync.dma_start(offsets[:], offs)
+        for q in range(4):
+            nc.sync.dma_start(tabs[32 * q : 32 * q + 4, :].bitcast(I32), tab_scales[0, 4 * q : 4 * q + 4, :].bitcast(I32))
+        nc.sync.dma_start(tabw[:], tab_words[0].rearrange("p n t -> p (n t)").bitcast(I32))
+        nc.sync.dma_start(temp[:], temper.rearrange("(p t) o -> p (t o)", t=PACK))
+        nc.sync.dma_start(dy_raw[:], dy.rearrange("(p j) c -> p j c", j=PACK))
+        nc.sync.dma_start(wo_raw[:], wo.rearrange("(p j) c -> p j c", j=PACK))
+        nc.sync.dma_start(old_sb[:], old.rearrange("(p t) c -> p t c", t=PACK))
+
+        def deal(engine, dst, raw, m0, m1):
+            src = raw[:].rearrange("p j (m t) -> p m j t", t=PACK)[:, m0:m1]
+            out = dst[:].rearrange("p t m j -> p m j t")[:, m0:m1]
+            if engine == "vector":
+                nc.vector.tensor_copy(out, src)
+            elif engine == "gpsimd":
+                nc.gpsimd.tensor_scalar(out, src, 1.0, 0.0, ALU.mult, ALU.add)
+            else:
+                nc.scalar.copy(out, src)
+
+        w1_bf = sb.tile([P, PACK, P, PACK], BF16, name="w1_bf", align_bytes=64)
+        w1_c = sb.tile([P, R], U32, name="w1_c", align_bytes=64)
+        w1_s = sb.tile([P, R], U8, name="w1_s", align_bytes=64)
+        gs = sb.tile([P, J], U8, name="gs", align_bytes=64)
+        deal("scalar", w1_bf, w1_raw, 0, 64)
+        deal("vector", w1_bf, w1_raw, 64, 128)
+        nc.vector.tensor_copy(gs[:], tabs[:].indirect(offsets[:]))
+        nc.vector.quantize_mx(out=w1_c[:].bitcast(FP8X4), scales=w1_s[:], in_=w1_bf[:].rearrange("p t m j -> p (t m j)"))
+        inv_t = sb.tile([P, PACK], F32, name="inv_t")
+        nc.vector.reciprocal(inv_t[:], temp[:])
+
+        gw = [sb.tile([P, HALF], U32, name="gw%d" % h, align_bytes=64) for h in range(2)]
+        for h in range(2):
+            nc.vector.tensor_copy(gw[h][:], tabw[:].bitcast(U32).indirect(offsets[:, 16 * h : 16 * (h + 1)]))
+
+        mx = sb.tile([P, PACK, G], F32, name="mx")
+        z = sb.tile([P, PACK, G], F32, name="z")
+        d = [sb.tile([P, PACK, HALF], F32, name="d%d" % h) for h in range(2)]
+        p = [sb.tile([P, PACK, HALF], F32, name="p%d" % h) for h in range(2)]
+        banks = {}
+        for h in range(2):
+            for u in range(2):
+                bank = ps.tile([P, 2, HALF], F32, name="a%d%d" % (h, u))
+                banks[h, u] = bank
+                for e in range(2):
+                    t = 2 * u + e
+                    nc.tensor.matmul_mx(
+                        out=bank[:, e, :],
+                        lhsT=w1_c[:, t * P : (t + 1) * P].bitcast(FP8X4), lhsT_scale=w1_s[:, t * P : (t + 1) * P],
+                        rhs=gw[h][:].bitcast(FP8X4), rhs_scale=gs[:, h * HALF : (h + 1) * HALF],
+                        start=True, stop=True)
+        for h in range(2):
+            gcols = slice(h * GH, (h + 1) * GH)
+            for u in range(2):
+                nc.vector.tensor_reduce(mx[:, 2 * u : 2 * u + 2, gcols], banks[h, u][:].rearrange("p e (g i) -> p e g i", i=POOL), AX.X, ALU.max)
+            for u in range(2):
+                nc.vector.tensor_tensor(
+                    d[h][:, 2 * u : 2 * u + 2, :].rearrange("p e (g i) -> p e g i", i=POOL),
+                    banks[h, u][:].rearrange("p e (g i) -> p e g i", i=POOL),
+                    mx[:, 2 * u : 2 * u + 2, gcols].unsqueeze(3).to_broadcast([P, 2, GH, POOL]),
+                    ALU.subtract)
+                for e in range(2):
+                    t = 2 * u + e
+                    nc.scalar.activation(p[h][:, t, :], d[h][:, t, :], ACT.Exp, scale=temp[:, t : t + 1])
+        for h in range(2):
+            gcols = slice(h * GH, (h + 1) * GH)
+            for u in range(2):
+                nc.vector.tensor_reduce(z[:, 2 * u : 2 * u + 2, gcols], p[h][:, 2 * u : 2 * u + 2, :].rearrange("p e (g i) -> p e g i", i=POOL), AX.X, ALU.add)
+
+        lnz = sb.tile([P, PACK, G], F32, name="lnz")
+        nc.scalar.activation(lnz[:], z[:], ACT.Ln)
+
+        wo_bf = sb.tile([P, PACK, P, PACK], BF16, name="wo_bf", align_bytes=64)
+        wo_c = sb.tile([P, R], U32, name="wo_c", align_bytes=64)
+        wo_s = sb.tile([P, R], U8, name="wo_s", align_bytes=64)
+        dy_bf = sb.tile([P, G, PACK], BF16, name="dy_bf", align_bytes=64)
+        dy_c = sb.tile([P, G], U32, name="dy_c", align_bytes=64)
+        dy_s = sb.tile([P, G], U8, name="dy_s", align_bytes=64)
+        deal("gpsimd", wo_bf, wo_raw, 0, 128)
+        nc.scalar.copy(dy_bf[:].rearrange("p (c i) j -> p c j i", i=4), dy_raw[:].rearrange("p j (c i) -> p c j i", i=4))
+        nc.vector.quantize_mx(out=wo_c[:].bitcast(FP8X4), scales=wo_s[:], in_=wo_bf[:].rearrange("p t m j -> p (t m j)"))
+        nc.vector.quantize_mx(out=dy_c[:].bitcast(FP8X4), scales=dy_s[:], in_=dy_bf[:].rearrange("p g j -> p (g j)"))
+        c0 = ps.tile([P, PACK, G], F32, name="c0")
+        for t in range(PACK):
+            nc.tensor.matmul_mx(
+                out=c0[:, t, :],
+                lhsT=wo_c[:, t * P : (t + 1) * P].bitcast(FP8X4), lhsT_scale=wo_s[:, t * P : (t + 1) * P],
+                rhs=dy_c[:].bitcast(FP8X4), rhs_scale=dy_s[:],
+                start=True, stop=True)
+
+        s = sb.tile([P, PACK, G], F32, name="s")
+        for t in range(PACK):
+            nc.vector.scalar_tensor_tensor(s[:, t, :], lnz[:, t, :], inv_t[:, t : t + 1], mx[:, t, :], ALU.mult, ALU.add)
+
+        rz = [sb.tile([P, PACK, GH], F32, name="rz%d" % h) for h in range(2)]
+        th = [sb.tile([P, PACK, GH], F32, name="th%d" % h) for h in range(2)]
+        cz = [sb.tile([P, PACK, GH], F32, name="cz%d" % h) for h in range(2)]
+        t1 = [sb.tile([P, PACK, GH], F32, name="t1%d" % h) for h in range(2)]
+        t2 = [sb.tile([P, PACK, GH], F32, name="t2%d" % h) for h in range(2)]
+        f = [sb.tile([P, PACK, GH], F32, name="f%d" % h) for h in range(2)]
+        for h in range(2):
+            gcols = slice(h * GH, (h + 1) * GH)
+            nc.scalar.activation(rz[h][:], lnz[:, :, gcols], ACT.Exp, scale=-1.0)
+            nc.scalar.activation(th[h][:], s[:, :, gcols], ACT.Tanh, scale=0.5)
+        for h in range(2):
+            gcols = slice(h * GH, (h + 1) * GH)
+            nc.vector.scalar_tensor_tensor(cz[h][:], c0[:, :, gcols], -0.25, rz[h][:], ALU.mult, ALU.mult)
+            nc.vector.scalar_tensor_tensor(t1[h][:], th[h][:], -1.0, s[:, :, gcols], ALU.add, ALU.mult)
+            nc.vector.scalar_tensor_tensor(t2[h][:], th[h][:], 1.0, cz[h][:], ALU.add, ALU.mult)
+        for h in range(2):
+            nc.vector.scalar_tensor_tensor(f[h][:], t1[h][:], -2.0, t2[h][:], ALU.add, ALU.mult)
+
+        da = [sb.tile([P, PACK, QUART], F32, name="da%d" % q) for q in range(4)]
+        y = [sb.tile([P, PACK, QUART], F32, name="y%d" % q) for q in range(4)]
+        y_bf = [sb.tile([P, QUART, PACK], BF16, name="y_bf%d" % q, align_bytes=64) for q in range(4)]
+        y_c = [sb.tile([P, QUART], I32, name="y_c%d" % q, align_bytes=64) for q in range(4)]
+        y_s = sb.tile([P, J], U8, name="y_s", align_bytes=64)
+        out_rows = out_0.rearrange("(p t) c -> p t c", t=PACK)
+        out_words = out_1[0].rearrange("p n t -> p (n t)").bitcast(I32)
+
+        def mul(q):
+            h, o = divmod(q, 2)
+            nc.vector.tensor_tensor(
+                da[q][:].rearrange("p t (g i) -> p t g i", i=POOL),
+                p[h][:, :, o * QUART : (o + 1) * QUART].rearrange("p t (g i) -> p t g i", i=POOL),
+                f[h][:, :, o * GQ : (o + 1) * GQ].unsqueeze(3).to_broadcast([P, PACK, GQ, POOL]),
+                ALU.mult)
+
+        def add(q):
+            cols = slice(q * QUART, (q + 1) * QUART)
+            nc.vector.tensor_tensor(y[q][:], da[q][:], old_sb[:, :, cols], ALU.add)
+            nc.sync.dma_start(out_rows[:, :, cols], y[q][:])
+            dst = y_bf[q][:].rearrange("p (c i) t -> p c t i", i=4)
+            src = y[q][:].rearrange("p t (c i) -> p c t i", i=4)
+            if q < 3:
+                nc.scalar.copy(dst, src)
+            else:
+                nc.vector.tensor_copy(dst, src)
+
+        def quant(q):
+            cols = slice(q * QUART, (q + 1) * QUART)
+            nc.vector.quantize_mx(out=y_c[q][:].bitcast(FP8X4), scales=y_s[:, cols], in_=y_bf[q][:].rearrange("p c t -> p (c t)"))
+            nc.sync.dma_start(out_words[:, cols], y_c[q][:])
+
+        mul(0)
+        mul(1)
+        add(0)
+        mul(2)
+        add(1)
+        mul(3)
+        add(2)
+        quant(0)
+        add(3)
+        quant(1)
+        quant(2)
+        quant(3)
+        for q in range(4):
+            eng = nc.sync if q % 2 == 0 else nc.scalar
+            eng.dma_start(out_2[0, 4 * q : 4 * q + 4, :].bitcast(I32), y_s[32 * q : 32 * q + 4, :].bitcast(I32))

@@ -56,8 +56,6 @@ def tile_attend_csoftmaxpool_pl_kernel(tc, tab_words, tab_scales, w1, temper, wo
             out = dst[:].rearrange("p t m j -> p m j t")[:, m0:m1]
             if engine == "vector":
                 nc.vector.tensor_copy(out, src)
-            elif engine == "gpsimd":
-                nc.gpsimd.tensor_scalar(out, src, 1.0, 0.0, ALU.mult, ALU.add)
             else:
                 nc.scalar.copy(out, src)
 
@@ -69,8 +67,6 @@ def tile_attend_csoftmaxpool_pl_kernel(tc, tab_words, tab_scales, w1, temper, wo
         deal("vector", w1_bf, w1_raw, 64, 128)
         nc.vector.tensor_copy(gs[:], tabs[:].indirect(offsets[:]))
         nc.vector.quantize_mx(out=w1_c[:].bitcast(FP8X4), scales=w1_s[:], in_=w1_bf[:].rearrange("p t m j -> p (t m j)"))
-        inv_t = sb.tile([P, PACK], F32, name="inv_t")
-        nc.vector.reciprocal(inv_t[:], temp[:])
 
         gw = [sb.tile([P, HALF], U32, name="gw%d" % h, align_bytes=64) for h in range(2)]
         for h in range(2):
@@ -96,15 +92,13 @@ def tile_attend_csoftmaxpool_pl_kernel(tc, tab_words, tab_scales, w1, temper, wo
             gcols = slice(h * GH, (h + 1) * GH)
             for u in range(2):
                 nc.vector.tensor_reduce(mx[:, 2 * u : 2 * u + 2, gcols], banks[h, u][:].rearrange("p e (g i) -> p e g i", i=POOL), AX.X, ALU.max)
-            for u in range(2):
+            for t in range(PACK):
                 nc.vector.tensor_tensor(
-                    d[h][:, 2 * u : 2 * u + 2, :].rearrange("p e (g i) -> p e g i", i=POOL),
-                    banks[h, u][:].rearrange("p e (g i) -> p e g i", i=POOL),
-                    mx[:, 2 * u : 2 * u + 2, gcols].unsqueeze(3).to_broadcast([P, 2, GH, POOL]),
+                    d[h][:, t, :].rearrange("p (g i) -> p g i", i=POOL),
+                    banks[h, t // 2][:, t % 2, :].rearrange("p (g i) -> p g i", i=POOL),
+                    mx[:, t, gcols].unsqueeze(2).to_broadcast([P, GH, POOL]),
                     ALU.subtract)
-                for e in range(2):
-                    t = 2 * u + e
-                    nc.scalar.activation(p[h][:, t, :], d[h][:, t, :], ACT.Exp, scale=temp[:, t : t + 1])
+                nc.scalar.activation(p[h][:, t, :], d[h][:, t, :], ACT.Exp, scale=temp[:, t : t + 1])
         for h in range(2):
             gcols = slice(h * GH, (h + 1) * GH)
             for u in range(2):
@@ -119,7 +113,9 @@ def tile_attend_csoftmaxpool_pl_kernel(tc, tab_words, tab_scales, w1, temper, wo
         dy_bf = sb.tile([P, G, PACK], BF16, name="dy_bf", align_bytes=64)
         dy_c = sb.tile([P, G], U32, name="dy_c", align_bytes=64)
         dy_s = sb.tile([P, G], U8, name="dy_s", align_bytes=64)
-        deal("gpsimd", wo_bf, wo_raw, 0, 128)
+        deal("scalar", wo_bf, wo_raw, 0, 16)
+        deal("scalar", wo_bf, wo_raw, 16, 32)
+        deal("vector", wo_bf, wo_raw, 32, 128)
         nc.scalar.copy(dy_bf[:].rearrange("p (c i) j -> p c j i", i=4), dy_raw[:].rearrange("p j (c i) -> p c j i", i=4))
         nc.vector.quantize_mx(out=wo_c[:].bitcast(FP8X4), scales=wo_s[:], in_=wo_bf[:].rearrange("p t m j -> p (t m j)"))
         nc.vector.quantize_mx(out=dy_c[:].bitcast(FP8X4), scales=dy_s[:], in_=dy_bf[:].rearrange("p g j -> p (g j)"))
@@ -131,6 +127,8 @@ def tile_attend_csoftmaxpool_pl_kernel(tc, tab_words, tab_scales, w1, temper, wo
                 rhs=dy_c[:].bitcast(FP8X4), rhs_scale=dy_s[:],
                 start=True, stop=True)
 
+        inv_t = sb.tile([P, PACK], F32, name="inv_t")
+        nc.vector.reciprocal(inv_t[:], temp[:])
         s = sb.tile([P, PACK, G], F32, name="s")
         for t in range(PACK):
             nc.vector.scalar_tensor_tensor(s[:, t, :], lnz[:, t, :], inv_t[:, t : t + 1], mx[:, t, :], ALU.mult, ALU.add)
@@ -153,37 +151,43 @@ def tile_attend_csoftmaxpool_pl_kernel(tc, tab_words, tab_scales, w1, temper, wo
         for h in range(2):
             nc.vector.scalar_tensor_tensor(f[h][:], t1[h][:], -2.0, t2[h][:], ALU.add, ALU.mult)
 
-        da = [sb.tile([P, PACK, QUART], F32, name="da%d" % q) for q in range(4)]
-        y = [sb.tile([P, PACK, QUART], F32, name="y%d" % q) for q in range(4)]
-        y_bf = [sb.tile([P, QUART, PACK], BF16, name="y_bf%d" % q, align_bytes=64) for q in range(4)]
-        y_c = [sb.tile([P, QUART], I32, name="y_c%d" % q, align_bytes=64) for q in range(4)]
+        widths = [128, 128, 128, 64, 64]
+        starts = [sum(widths[:q]) for q in range(len(widths))]
+        last = len(widths) - 1
+        da = [sb.tile([P, PACK, w], F32, name="da%d" % q) for q, w in enumerate(widths)]
+        y = [sb.tile([P, PACK, w], F32, name="y%d" % q) for q, w in enumerate(widths)]
+        y_bf = [sb.tile([P, w, PACK], BF16, name="y_bf%d" % q, align_bytes=64) for q, w in enumerate(widths)]
+        y_c = sb.tile([P, J], I32, name="y_c", align_bytes=64)
         y_s = sb.tile([P, J], U8, name="y_s", align_bytes=64)
         out_rows = out_0.rearrange("(p t) c -> p t c", t=PACK)
         out_words = out_1[0].rearrange("p n t -> p (n t)").bitcast(I32)
 
         def mul(q):
-            h, o = divmod(q, 2)
+            h, o = divmod(starts[q], HALF)
+            w = widths[q]
             nc.vector.tensor_tensor(
                 da[q][:].rearrange("p t (g i) -> p t g i", i=POOL),
-                p[h][:, :, o * QUART : (o + 1) * QUART].rearrange("p t (g i) -> p t g i", i=POOL),
-                f[h][:, :, o * GQ : (o + 1) * GQ].unsqueeze(3).to_broadcast([P, PACK, GQ, POOL]),
+                p[h][:, :, o : o + w].rearrange("p t (g i) -> p t g i", i=POOL),
+                f[h][:, :, o // POOL : (o + w) // POOL].unsqueeze(3).to_broadcast([P, PACK, w // POOL, POOL]),
                 ALU.mult)
 
         def add(q):
-            cols = slice(q * QUART, (q + 1) * QUART)
+            cols = slice(starts[q], starts[q] + widths[q])
             nc.vector.tensor_tensor(y[q][:], da[q][:], old_sb[:, :, cols], ALU.add)
             nc.sync.dma_start(out_rows[:, :, cols], y[q][:])
             dst = y_bf[q][:].rearrange("p (c i) t -> p c t i", i=4)
             src = y[q][:].rearrange("p t (c i) -> p c t i", i=4)
-            if q < 3:
+            if q < last:
                 nc.scalar.copy(dst, src)
             else:
                 nc.vector.tensor_copy(dst, src)
 
         def quant(q):
-            cols = slice(q * QUART, (q + 1) * QUART)
-            nc.vector.quantize_mx(out=y_c[q][:].bitcast(FP8X4), scales=y_s[:, cols], in_=y_bf[q][:].rearrange("p c t -> p (c t)"))
-            nc.sync.dma_start(out_words[:, cols], y_c[q][:])
+            cols = slice(starts[q], starts[q] + widths[q])
+            nc.vector.quantize_mx(out=y_c[:, cols].bitcast(FP8X4), scales=y_s[:, cols], in_=y_bf[q][:].rearrange("p c t -> p (c t)"))
+
+        def store_words(a, b):
+            nc.scalar.dma_start(out_words[:, a:b], y_c[:, a:b])
 
         mul(0)
         mul(1)
@@ -193,10 +197,15 @@ def tile_attend_csoftmaxpool_pl_kernel(tc, tab_words, tab_scales, w1, temper, wo
         mul(3)
         add(2)
         quant(0)
+        mul(4)
         add(3)
         quant(1)
+        add(4)
         quant(2)
+        store_words(0, 384)
         quant(3)
+        quant(4)
+        store_words(384, 512)
         for q in range(4):
-            eng = nc.sync if q % 2 == 0 else nc.scalar
+            eng = nc.sync if q < 3 else nc.scalar
             eng.dma_start(out_2[0, 4 * q : 4 * q + 4, :].bitcast(I32), y_s[32 * q : 32 * q + 4, :].bitcast(I32))

@@ -52,8 +52,8 @@ def tile_attend_csoftmaxpool_pl_kernel(tc, tab_words, tab_scales, w1, temper, wo
         nc.sync.dma_start(old_sb[:], old.rearrange("(p t) c -> p t c", t=PACK))
 
         def deal(engine, dst, raw, m0, m1):
-            src = raw[:].rearrange("p j (m t) -> p m j t", t=PACK)[:, m0:m1]
-            out = dst[:].rearrange("p t m j -> p m j t")[:, m0:m1]
+            src = raw[:].rearrange("p j (m t) -> p m t j", t=PACK)[:, m0:m1]
+            out = dst[:].rearrange("p t m j -> p m t j")[:, m0:m1]
             if engine == "vector":
                 nc.vector.tensor_copy(out, src)
             else:
@@ -116,7 +116,7 @@ def tile_attend_csoftmaxpool_pl_kernel(tc, tab_words, tab_scales, w1, temper, wo
         deal("scalar", wo_bf, wo_raw, 0, 16)
         deal("scalar", wo_bf, wo_raw, 16, 32)
         deal("vector", wo_bf, wo_raw, 32, 128)
-        nc.scalar.copy(dy_bf[:].rearrange("p (c i) j -> p c j i", i=4), dy_raw[:].rearrange("p j (c i) -> p c j i", i=4))
+        nc.scalar.copy(dy_bf[:], dy_raw[:].rearrange("p j g -> p g j"))
         nc.vector.quantize_mx(out=wo_c[:].bitcast(FP8X4), scales=wo_s[:], in_=wo_bf[:].rearrange("p t m j -> p (t m j)"))
         nc.vector.quantize_mx(out=dy_c[:].bitcast(FP8X4), scales=dy_s[:], in_=dy_bf[:].rearrange("p g j -> p (g j)"))
         c0 = ps.tile([P, PACK, G], F32, name="c0")
@@ -175,8 +175,8 @@ def tile_attend_csoftmaxpool_pl_kernel(tc, tab_words, tab_scales, w1, temper, wo
             cols = slice(starts[q], starts[q] + widths[q])
             nc.vector.tensor_tensor(y[q][:], da[q][:], old_sb[:, :, cols], ALU.add)
             nc.sync.dma_start(out_rows[:, :, cols], y[q][:])
-            dst = y_bf[q][:].rearrange("p (c i) t -> p c t i", i=4)
-            src = y[q][:].rearrange("p t (c i) -> p c t i", i=4)
+            dst = y_bf[q][:]
+            src = y[q][:].rearrange("p t c -> p c t")
             if q < last:
                 nc.scalar.copy(dst, src)
             else:

@@ -1,6 +1,8 @@
+import math
 from contextlib import ExitStack
 
 import concourse.mybir as mybir
+from concourse.masks import make_identity
 
 K, R, F, T, J, G = 512, 512, 512, 2048, 512, 128
 FLOPS = 2 * K * R * J + 2 * F * R * G
@@ -32,7 +34,7 @@ def tile_attend_csoftmaxpool_pl_kernel(tc, tab_words, tab_scales, w1, temper, wo
         ps = ctx.enter_context(tc.psum_pool(name="ps", bufs=1))
 
         offsets = sb.tile([P, J // 16], U16, name="offsets")
-        tabw = sb.tile([P, T], I32, name="tabw", align_bytes=64)
+        tabw = sb.tile([P, T], I32, name="tabw", tag="tabw", align_bytes=64)
         tabs = sb.tile([P, T], U8, name="tabs", align_bytes=64)
         w1_raw = sb.tile([P, PACK, R], F32, name="w1_raw")
         wo_raw = sb.tile([P, PACK, R], F32, name="wo_raw")
@@ -51,30 +53,36 @@ def tile_attend_csoftmaxpool_pl_kernel(tc, tab_words, tab_scales, w1, temper, wo
         nc.sync.dma_start(wo_raw[:], wo.rearrange("(p j) c -> p j c", j=PACK))
         nc.sync.dma_start(old_sb[:], old.rearrange("(p t) c -> p t c", t=PACK))
 
+        ident = sb.tile([P, P], F32, name="ident")
+        make_identity(nc, ident[:])
+
         def deal(engine, dst, raw, m0, m1):
             src = raw[:].rearrange("p j (m t) -> p m t j", t=PACK)[:, m0:m1]
             out = dst[:].rearrange("p t m j -> p m t j")[:, m0:m1]
             if engine == "vector":
                 nc.vector.tensor_copy(out, src)
+            elif engine == "gpsimd":
+                nc.gpsimd.tensor_scalar(out, src, 1.0, 0.0, ALU.mult, ALU.add)
             else:
                 nc.scalar.copy(out, src)
 
         w1_bf = sb.tile([P, PACK, P, PACK], BF16, name="w1_bf", align_bytes=64)
         w1_c = sb.tile([P, R], U32, name="w1_c", align_bytes=64)
         w1_s = sb.tile([P, R], U8, name="w1_s", align_bytes=64)
-        gs = sb.tile([P, J], U8, name="gs", align_bytes=64)
-        deal("scalar", w1_bf, w1_raw, 0, 64)
-        deal("vector", w1_bf, w1_raw, 64, 128)
-        nc.vector.tensor_copy(gs[:], tabs[:].indirect(offsets[:]))
+        deal("scalar", w1_bf, w1_raw, 0, 40)
+        deal("vector", w1_bf, w1_raw, 40, 128)
         nc.vector.quantize_mx(out=w1_c[:].bitcast(FP8X4), scales=w1_s[:], in_=w1_bf[:].rearrange("p t m j -> p (t m j)"))
 
         gw = [sb.tile([P, HALF], U32, name="gw%d" % h, align_bytes=64) for h in range(2)]
+        gs = [sb.tile([P, HALF], U8, name="gs0", align_bytes=64)]
+        nc.vector.tensor_copy(gs[0][:], tabs[:].indirect(offsets[:, :16]))
         for h in range(2):
             nc.vector.tensor_copy(gw[h][:], tabw[:].bitcast(U32).indirect(offsets[:, 16 * h : 16 * (h + 1)]))
+        gs.append(sb.tile([P, HALF], U8, name="gs1", tag="tabw", align_bytes=64))
+        nc.vector.tensor_copy(gs[1][:], tabs[:].indirect(offsets[:, 16:]))
 
-        mx = sb.tile([P, PACK, G], F32, name="mx")
-        z = sb.tile([P, PACK, G], F32, name="z")
-        d = [sb.tile([P, PACK, HALF], F32, name="d%d" % h) for h in range(2)]
+        mx = [sb.tile([P, PACK, GH], F32, name="mx%d" % h) for h in range(2)]
+        d = [sb.tile([P, PACK, HALF], F32, name="d%d" % h, tag="d%d" % h, align_bytes=64) for h in range(2)]
         p = [sb.tile([P, PACK, HALF], F32, name="p%d" % h) for h in range(2)]
         banks = {}
         for h in range(2):
@@ -86,26 +94,31 @@ def tile_attend_csoftmaxpool_pl_kernel(tc, tab_words, tab_scales, w1, temper, wo
                     nc.tensor.matmul_mx(
                         out=bank[:, e, :],
                         lhsT=w1_c[:, t * P : (t + 1) * P].bitcast(FP8X4), lhsT_scale=w1_s[:, t * P : (t + 1) * P],
-                        rhs=gw[h][:].bitcast(FP8X4), rhs_scale=gs[:, h * HALF : (h + 1) * HALF],
+                        rhs=gw[h][:].bitcast(FP8X4), rhs_scale=gs[h][:],
                         start=True, stop=True)
+        zt = ps.tile([P, 4, P], F32, name="zt")
         for h in range(2):
-            gcols = slice(h * GH, (h + 1) * GH)
             for u in range(2):
-                nc.vector.tensor_reduce(mx[:, 2 * u : 2 * u + 2, gcols], banks[h, u][:].rearrange("p e (g i) -> p e g i", i=POOL), AX.X, ALU.max)
+                nc.vector.tensor_reduce(mx[h][:, 2 * u : 2 * u + 2, :], banks[h, u][:].rearrange("p e (g i) -> p e g i", i=POOL), AX.X, ALU.max)
             for t in range(PACK):
                 nc.vector.tensor_tensor(
                     d[h][:, t, :].rearrange("p (g i) -> p g i", i=POOL),
                     banks[h, t // 2][:, t % 2, :].rearrange("p (g i) -> p g i", i=POOL),
-                    mx[:, t, gcols].unsqueeze(2).to_broadcast([P, GH, POOL]),
+                    mx[h][:, t, :].unsqueeze(2).to_broadcast([P, GH, POOL]),
                     ALU.subtract)
                 nc.scalar.activation(p[h][:, t, :], d[h][:, t, :], ACT.Exp, scale=temp[:, t : t + 1])
         for h in range(2):
-            gcols = slice(h * GH, (h + 1) * GH)
             for u in range(2):
-                nc.vector.tensor_reduce(z[:, 2 * u : 2 * u + 2, gcols], p[h][:, 2 * u : 2 * u + 2, :].rearrange("p e (g i) -> p e g i", i=POOL), AX.X, ALU.add)
+                members = p[h][:, 2 * u : 2 * u + 2, :].rearrange("p e (g i) -> p (e g) i", i=POOL)
+                for i in range(POOL):
+                    nc.tensor.matmul(zt[:, 2 * h + u, :], members[:, :, i], ident[:], start=(i == 0), stop=(i == POOL - 1), is_transpose=True)
 
-        lnz = sb.tile([P, PACK, G], F32, name="lnz")
-        nc.scalar.activation(lnz[:], z[:], ACT.Ln)
+        lnzt = sb.tile([P, 4, P], F32, name="lnzt")
+        nc.scalar.activation(lnzt[:], zt[:], ACT.Ln)
+        lnz = ps.tile([P, 2, PACK, GH], F32, name="lnz")
+        for h in range(2):
+            for u in range(2):
+                nc.tensor.transpose(lnz[:, h, 2 * u : 2 * u + 2, :].rearrange("p e g -> p (e g)"), lnzt[:, 2 * h + u, :], ident[:])
 
         wo_bf = sb.tile([P, PACK, P, PACK], BF16, name="wo_bf", align_bytes=64)
         wo_c = sb.tile([P, R], U32, name="wo_c", align_bytes=64)
@@ -113,9 +126,7 @@ def tile_attend_csoftmaxpool_pl_kernel(tc, tab_words, tab_scales, w1, temper, wo
         dy_bf = sb.tile([P, G, PACK], BF16, name="dy_bf", align_bytes=64)
         dy_c = sb.tile([P, G], U32, name="dy_c", align_bytes=64)
         dy_s = sb.tile([P, G], U8, name="dy_s", align_bytes=64)
-        deal("scalar", wo_bf, wo_raw, 0, 16)
-        deal("scalar", wo_bf, wo_raw, 16, 32)
-        deal("vector", wo_bf, wo_raw, 32, 128)
+        deal("gpsimd", wo_bf, wo_raw, 0, P)
         nc.scalar.copy(dy_bf[:], dy_raw[:].rearrange("p j g -> p g j"))
         nc.vector.quantize_mx(out=wo_c[:].bitcast(FP8X4), scales=wo_s[:], in_=wo_bf[:].rearrange("p t m j -> p (t m j)"))
         nc.vector.quantize_mx(out=dy_c[:].bitcast(FP8X4), scales=dy_s[:], in_=dy_bf[:].rearrange("p g j -> p (g j)"))
@@ -129,25 +140,34 @@ def tile_attend_csoftmaxpool_pl_kernel(tc, tab_words, tab_scales, w1, temper, wo
 
         inv_t = sb.tile([P, PACK], F32, name="inv_t")
         nc.vector.reciprocal(inv_t[:], temp[:])
-        s = sb.tile([P, PACK, G], F32, name="s")
-        for t in range(PACK):
-            nc.vector.scalar_tensor_tensor(s[:, t, :], lnz[:, t, :], inv_t[:, t : t + 1], mx[:, t, :], ALU.mult, ALU.add)
+        s = [sb.tile([P, PACK, GH], F32, name="s%d" % h) for h in range(2)]
+        for h in range(2):
+            for t in range(PACK):
+                nc.vector.scalar_tensor_tensor(s[h][:, t, :], lnz[:, h, t, :], inv_t[:, t : t + 1], mx[h][:, t, :], ALU.mult, ALU.add)
+
+        pc = [sb.tile([P, PACK, HALF], F32, name="pc%d" % h) for h in range(2)]
+        for h in range(2):
+            for u in range(2):
+                rows = slice(2 * u, 2 * u + 2)
+                nc.vector.tensor_tensor(
+                    pc[h][:, rows, :].rearrange("p e (g i) -> p e g i", i=POOL),
+                    p[h][:, rows, :].rearrange("p e (g i) -> p e g i", i=POOL),
+                    c0[:, rows, h * GH : (h + 1) * GH].unsqueeze(3).to_broadcast([P, 2, GH, POOL]),
+                    ALU.mult)
 
         rz = [sb.tile([P, PACK, GH], F32, name="rz%d" % h) for h in range(2)]
         th = [sb.tile([P, PACK, GH], F32, name="th%d" % h) for h in range(2)]
-        cz = [sb.tile([P, PACK, GH], F32, name="cz%d" % h) for h in range(2)]
         t1 = [sb.tile([P, PACK, GH], F32, name="t1%d" % h) for h in range(2)]
         t2 = [sb.tile([P, PACK, GH], F32, name="t2%d" % h) for h in range(2)]
         f = [sb.tile([P, PACK, GH], F32, name="f%d" % h) for h in range(2)]
         for h in range(2):
             gcols = slice(h * GH, (h + 1) * GH)
-            nc.scalar.activation(rz[h][:], lnz[:, :, gcols], ACT.Exp, scale=-1.0)
-            nc.scalar.activation(th[h][:], s[:, :, gcols], ACT.Tanh, scale=0.5)
+            nc.scalar.activation(th[h][:], s[h][:], ACT.Tanh, scale=0.5)
+            nc.scalar.activation(rz[h][:], lnz[:, h], ACT.Exp, scale=-1.0, bias=-math.log(4.0))
         for h in range(2):
             gcols = slice(h * GH, (h + 1) * GH)
-            nc.vector.scalar_tensor_tensor(cz[h][:], c0[:, :, gcols], -0.25, rz[h][:], ALU.mult, ALU.mult)
-            nc.vector.scalar_tensor_tensor(t1[h][:], th[h][:], -1.0, s[:, :, gcols], ALU.add, ALU.mult)
-            nc.vector.scalar_tensor_tensor(t2[h][:], th[h][:], 1.0, cz[h][:], ALU.add, ALU.mult)
+            nc.vector.scalar_tensor_tensor(t1[h][:], th[h][:], -1.0, s[h][:], ALU.add, ALU.mult)
+            nc.vector.scalar_tensor_tensor(t2[h][:], th[h][:], 1.0, rz[h][:], ALU.add, ALU.mult)
         for h in range(2):
             nc.vector.scalar_tensor_tensor(f[h][:], t1[h][:], -2.0, t2[h][:], ALU.add, ALU.mult)
 
@@ -167,13 +187,13 @@ def tile_attend_csoftmaxpool_pl_kernel(tc, tab_words, tab_scales, w1, temper, wo
             w = widths[q]
             nc.vector.tensor_tensor(
                 da[q][:].rearrange("p t (g i) -> p t g i", i=POOL),
-                p[h][:, :, o : o + w].rearrange("p t (g i) -> p t g i", i=POOL),
+                pc[h][:, :, o : o + w].rearrange("p t (g i) -> p t g i", i=POOL),
                 f[h][:, :, o // POOL : (o + w) // POOL].unsqueeze(3).to_broadcast([P, PACK, w // POOL, POOL]),
                 ALU.mult)
 
         def add(q):
             cols = slice(starts[q], starts[q] + widths[q])
-            nc.vector.tensor_tensor(y[q][:], da[q][:], old_sb[:, :, cols], ALU.add)
+            nc.vector.tensor_tensor(y[q][:], old_sb[:, :, cols], da[q][:], ALU.subtract)
             nc.sync.dma_start(out_rows[:, :, cols], y[q][:])
             dst = y_bf[q][:]
             src = y[q][:].rearrange("p t c -> p c t")

import math
from contextlib import ExitStack

import concourse.mybir as mybir
from concourse.masks import make_identity

K, R, F, T, J, G = 512, 512, 512, 2048, 512, 128
FLOPS = 2 * K * R * J + 2 * F * R * G

F32 = mybir.dt.float32
BF16 = mybir.dt.bfloat16
I32 = mybir.dt.int32
U32 = mybir.dt.uint32
U16 = mybir.dt.uint16
U8 = mybir.dt.uint8
FP8X4 = mybir.dt.float8_e4m3fn_x4
ALU = mybir.AluOpType
ACT = mybir.ActivationFunctionType
AX = mybir.AxisListType

P = 128
PACK = 4
POOL = J // G
HALF = J // 2
GH = G // 2
QUART = J // 4
GQ = G // 4


def tile_attend_csoftmaxpool_pl_kernel(tc, tab_words, tab_scales, w1, temper, wo, dy, old, offs, out_0, out_1, out_2):
    nc = tc.nc
    with ExitStack() as ctx:
        sb = ctx.enter_context(tc.tile_pool(name="sb", bufs=1))
        ps = ctx.enter_context(tc.psum_pool(name="ps", bufs=1))

        offsets = sb.tile([P, J // 16], U16, name="offsets")
        tabw = sb.tile([P, T], I32, name="tabw", tag="tabw", align_bytes=64)
        tabs = sb.tile([P, T], U8, name="tabs", align_bytes=64)
        w1_raw = sb.tile([P, PACK, R], F32, name="w1_raw")
        wo_raw = sb.tile([P, PACK, R], F32, name="wo_raw")
        dy_raw = sb.tile([P, PACK, G], F32, name="dy_raw")
        old_sb = sb.tile([P, PACK, J], F32, name="old_sb")
        temp = sb.tile([P, PACK], F32, name="temp")

        nc.vector.memset(tabs[:].bitcast(I32), 0)
        nc.sync.dma_start(w1_raw[:], w1.rearrange("(p j) c -> p j c", j=PACK))
        nc.sync.dma_start(offsets[:], offs)
        for q in range(4):
            nc.sync.dma_start(tabs[32 * q : 32 * q + 4, :].bitcast(I32), tab_scales[0, 4 * q : 4 * q + 4, :].bitcast(I32))
        nc.sync.dma_start(tabw[:], tab_words[0].rearrange("p n t -> p (n t)").bitcast(I32))
        nc.sync.dma_start(temp[:], temper.rearrange("(p t) o -> p (t o)", t=PACK))
        nc.sync.dma_start(dy_raw[:], dy.rearrange("(p j) c -> p j c", j=PACK))
        nc.sync.dma_start(wo_raw[:], wo.rearrange("(p j) c -> p j c", j=PACK))
        nc.sync.dma_start(old_sb[:], old.rearrange("(p t) c -> p t c", t=PACK))

        ident = sb.tile([P, P], F32, name="ident")
        make_identity(nc, ident[:])

        def deal(engine, dst, raw, m0, m1):
            src = raw[:].rearrange("p j (m t) -> p m t j", t=PACK)[:, m0:m1]
            out = dst[:].rearrange("p t m j -> p m t j")[:, m0:m1]
            if engine == "vector":
                nc.vector.tensor_copy(out, src)
            elif engine == "gpsimd":
                nc.gpsimd.tensor_scalar(out, src, 1.0, 0.0, ALU.mult, ALU.add)
            else:
                nc.scalar.copy(out, src)

        w1_bf = sb.tile([P, PACK, P, PACK], BF16, name="w1_bf", align_bytes=64)
        w1_c = sb.tile([P, R], U32, name="w1_c", align_bytes=64)
        w1_s = sb.tile([P, R], U8, name="w1_s", align_bytes=64)
        deal("scalar", w1_bf, w1_raw, 0, 40)
        deal("vector", w1_bf, w1_raw, 40, 128)
        nc.vector.quantize_mx(out=w1_c[:].bitcast(FP8X4), scales=w1_s[:], in_=w1_bf[:].rearrange("p t m j -> p (t m j)"))

        gw = [sb.tile([P, HALF], U32, name="gw%d" % h, align_bytes=64) for h in range(2)]
        gs = [sb.tile([P, HALF], U8, name="gs0", align_bytes=64)]
        nc.vector.tensor_copy(gs[0][:], tabs[:].indirect(offsets[:, :16]))
        for h in range(2):
            nc.vector.tensor_copy(gw[h][:], tabw[:].bitcast(U32).indirect(offsets[:, 16 * h : 16 * (h + 1)]))
        gs.append(sb.tile([P, HALF], U8, name="gs1", tag="tabw", align_bytes=64))
        nc.vector.tensor_copy(gs[1][:], tabs[:].indirect(offsets[:, 16:]))

        mx = [sb.tile([P, PACK, GH], F32, name="mx%d" % h) for h in range(2)]
        d = [sb.tile([P, PACK, HALF], F32, name="d%d" % h, tag="d%d" % h, align_bytes=64) for h in range(2)]
        p = [sb.tile([P, PACK, HALF], F32, name="p%d" % h) for h in range(2)]
        banks = {}
        for h in range(2):
            for u in range(2):
                bank = ps.tile([P, 2, HALF], F32, name="a%d%d" % (h, u))
                banks[h, u] = bank
                for e in range(2):
                    t = 2 * u + e
                    nc.tensor.matmul_mx(
                        out=bank[:, e, :],
                        lhsT=w1_c[:, t * P : (t + 1) * P].bitcast(FP8X4), lhsT_scale=w1_s[:, t * P : (t + 1) * P],
                        rhs=gw[h][:].bitcast(FP8X4), rhs_scale=gs[h][:],
                        start=True, stop=True)
        zt = ps.tile([P, 4, P], F32, name="zt")
        for h in range(2):
            for u in range(2):
                nc.vector.tensor_reduce(mx[h][:, 2 * u : 2 * u + 2, :], banks[h, u][:].rearrange("p e (g i) -> p e g i", i=POOL), AX.X, ALU.max)
            for t in range(PACK):
                nc.vector.tensor_tensor(
                    d[h][:, t, :].rearrange("p (g i) -> p g i", i=POOL),
                    banks[h, t // 2][:, t % 2, :].rearrange("p (g i) -> p g i", i=POOL),
                    mx[h][:, t, :].unsqueeze(2).to_broadcast([P, GH, POOL]),
                    ALU.subtract)
                nc.scalar.activation(p[h][:, t, :], d[h][:, t, :], ACT.Exp, scale=temp[:, t : t + 1])
        for h in range(2):
            for u in range(2):
                members = p[h][:, 2 * u : 2 * u + 2, :].rearrange("p e (g i) -> p (e g) i", i=POOL)
                for i in range(POOL):
                    nc.tensor.matmul(zt[:, 2 * h + u, :], members[:, :, i], ident[:], start=(i == 0), stop=(i == POOL - 1), is_transpose=True)

        lnzt = sb.tile([P, 4, P], F32, name="lnzt")
        nc.scalar.activation(lnzt[:], zt[:], ACT.Ln)
        lnz = ps.tile([P, 2, PACK, GH], F32, name="lnz")
        for h in range(2):
            for u in range(2):
                nc.tensor.transpose(lnz[:, h, 2 * u : 2 * u + 2, :].rearrange("p e g -> p (e g)"), lnzt[:, 2 * h + u, :], ident[:])

        wo_bf = sb.tile([P, PACK, P, PACK], BF16, name="wo_bf", align_bytes=64)
        wo_c = sb.tile([P, R], U32, name="wo_c", align_bytes=64)
        wo_s = sb.tile([P, R], U8, name="wo_s", align_bytes=64)
        dy_bf = sb.tile([P, G, PACK], BF16, name="dy_bf", align_bytes=64)
        dy_c = sb.tile([P, G], U32, name="dy_c", align_bytes=64)
        dy_s = sb.tile([P, G], U8, name="dy_s", align_bytes=64)
        deal("gpsimd", wo_bf, wo_raw, 0, P)
        nc.scalar.copy(dy_bf[:], dy_raw[:].rearrange("p j g -> p g j"))
        nc.vector.quantize_mx(out=wo_c[:].bitcast(FP8X4), scales=wo_s[:], in_=wo_bf[:].rearrange("p t m j -> p (t m j)"))
        nc.vector.quantize_mx(out=dy_c[:].bitcast(FP8X4), scales=dy_s[:], in_=dy_bf[:].rearrange("p g j -> p (g j)"))
        c0 = ps.tile([P, PACK, G], F32, name="c0")
        for t in range(PACK):
            nc.tensor.matmul_mx(
                out=c0[:, t, :],
                lhsT=wo_c[:, t * P : (t + 1) * P].bitcast(FP8X4), lhsT_scale=wo_s[:, t * P : (t + 1) * P],
                rhs=dy_c[:].bitcast(FP8X4), rhs_scale=dy_s[:],
                start=True, stop=True)

        inv_t = sb.tile([P, PACK], F32, name="inv_t")
        nc.vector.reciprocal(inv_t[:], temp[:])
        s = [sb.tile([P, PACK, GH], F32, name="s%d" % h) for h in range(2)]
        for h in range(2):
            for t in range(PACK):
                nc.vector.scalar_tensor_tensor(s[h][:, t, :], lnz[:, h, t, :], inv_t[:, t : t + 1], mx[h][:, t, :], ALU.mult, ALU.add)

        pc = [sb.tile([P, PACK, HALF], F32, name="pc%d" % h) for h in range(2)]
        for h in range(2):
            for u in range(2):
                rows = slice(2 * u, 2 * u + 2)
                nc.vector.tensor_tensor(
                    pc[h][:, rows, :].rearrange("p e (g i) -> p e g i", i=POOL),
                    p[h][:, rows, :].rearrange("p e (g i) -> p e g i", i=POOL),
                    c0[:, rows, h * GH : (h + 1) * GH].unsqueeze(3).to_broadcast([P, 2, GH, POOL]),
                    ALU.mult)

        rz = [sb.tile([P, PACK, GH], F32, name="rz%d" % h) for h in range(2)]
        th = [sb.tile([P, PACK, GH], F32, name="th%d" % h) for h in range(2)]
        t1 = [sb.tile([P, PACK, GH], F32, name="t1%d" % h) for h in range(2)]
        t2 = [sb.tile([P, PACK, GH], F32, name="t2%d" % h) for h in range(2)]
        f = [sb.tile([P, PACK, GH], F32, name="f%d" % h) for h in range(2)]
        for h in range(2):
            gcols = slice(h * GH, (h + 1) * GH)
            nc.scalar.activation(th[h][:], s[h][:], ACT.Tanh, scale=0.5)
            nc.scalar.activation(rz[h][:], lnz[:, h], ACT.Exp, scale=-1.0, bias=-math.log(4.0))
        for h in range(2):
            gcols = slice(h * GH, (h + 1) * GH)
            nc.vector.scalar_tensor_tensor(t1[h][:], th[h][:], -1.0, s[h][:], ALU.add, ALU.mult)
            nc.vector.scalar_tensor_tensor(t2[h][:], th[h][:], 1.0, rz[h][:], ALU.add, ALU.mult)
        for h in range(2):
            nc.vector.scalar_tensor_tensor(f[h][:], t1[h][:], -2.0, t2[h][:], ALU.add, ALU.mult)

        widths = [128, 128, 128, 64, 64]
        starts = [sum(widths[:q]) for q in range(len(widths))]
        last = len(widths) - 1
        da = [sb.tile([P, PACK, w], F32, name="da%d" % q) for q, w in enumerate(widths)]
        y = [sb.tile([P, PACK, w], F32, name="y%d" % q) for q, w in enumerate(widths)]
        y_bf = [sb.tile([P, w, PACK], BF16, name="y_bf%d" % q, align_bytes=64) for q, w in enumerate(widths)]
        y_c = sb.tile([P, J], I32, name="y_c", align_bytes=64)
        y_s = sb.tile([P, J], U8, name="y_s", align_bytes=64)
        out_rows = out_0.rearrange("(p t) c -> p t c", t=PACK)
        out_words = out_1[0].rearrange("p n t -> p (n t)").bitcast(I32)

        def mul(q):
            h, o = divmod(starts[q], HALF)
            w = widths[q]
            nc.vector.tensor_tensor(
                da[q][:].rearrange("p t (g i) -> p t g i", i=POOL),
                pc[h][:, :, o : o + w].rearrange("p t (g i) -> p t g i", i=POOL),
                f[h][:, :, o // POOL : (o + w) // POOL].unsqueeze(3).to_broadcast([P, PACK, w // POOL, POOL]),
                ALU.mult)

        def add(q):
            cols = slice(starts[q], starts[q] + widths[q])
            nc.vector.tensor_tensor(y[q][:], old_sb[:, :, cols], da[q][:], ALU.subtract)
            nc.sync.dma_start(out_rows[:, :, cols], y[q][:])
            dst = y_bf[q][:]
            src = y[q][:].rearrange("p t c -> p c t")
            if q < last:
                nc.scalar.copy(dst, src)
            else:
                nc.vector.tensor_copy(dst, src)

        def quant(q):
            cols = slice(starts[q], starts[q] + widths[q])
            nc.vector.quantize_mx(out=y_c[:, cols].bitcast(FP8X4), scales=y_s[:, cols], in_=y_bf[q][:].rearrange("p c t -> p (c t)"))

        def store_words(a, b):
            nc.scalar.dma_start(out_words[:, a:b], y_c[:, a:b])

        mul(0)
        mul(1)
        add(0)
        mul(2)
        add(1)
        mul(3)
        add(2)
        quant(0)
        mul(4)
        add(3)
        quant(1)
        add(4)
        quant(2)
        store_words(0, 384)
        quant(3)
        quant(4)
        store_words(384, 512)
        for q in range(4):
            eng = nc.sync if q < 3 else nc.scalar
            eng.dma_start(out_2[0, 4 * q : 4 * q + 4, :].bitcast(I32), y_s[32 * q : 32 * q + 4, :].bitcast(I32))
